import numpy as np
import ml_dtypes


def mxq(x, axis, fmt="e4m3"):
    dtype, down = {"e4m3": (ml_dtypes.float8_e4m3fn, 7), "e5m2": (ml_dtypes.float8_e5m2, 14)}[fmt]
    v = np.moveaxis(np.asarray(x, np.float32).astype(ml_dtypes.bfloat16).astype(np.float64), axis, -1)
    blocks = v.reshape(v.shape[:-1] + (-1, 32))
    amax = np.abs(blocks).max(-1, keepdims=True)
    byte = np.maximum(np.where(amax > 0, np.frexp(amax)[1] - 1 + 127, 0) - down, 1)
    scale = np.exp2(byte - 127.0)
    codes = (blocks / scale).astype(np.float32).astype(dtype).astype(np.float64)
    return np.moveaxis((codes * scale).reshape(v.shape), -1, axis)


WIDE = False


def mx_kscale(k):
    if not WIDE:
        return np.ones(k)
    levels = np.array([10, -10, 5, -5, 0])
    if k % 512:
        return np.exp2(np.random.permutation(np.resize(levels, k // 32))).repeat(32)
    a = np.empty((k // 512, 16))
    for p in range(k // 512):
        a[p, :8] = np.random.permutation(np.resize(levels, 8))
        for g in range(8):
            far = levels[np.abs(levels - a[p, g]) >= 10]
            a[p, g + 8] = far[np.random.randint(len(far))]
    return np.exp2(a.ravel()).repeat(32)


def f64(x):
    return np.asarray(x).astype(np.float64)


def striped(idx):
    return np.tile(idx.reshape(-1, 16).T, (8, 1)).astype(np.uint16)


def unstriped(offs):
    return offs[:16].T.reshape(-1).astype(np.int64)


def striped8(idx):
    return np.concatenate([x.reshape(-1, 16).T for x in idx]).astype(np.uint16)


def runs(offs, k):
    lists = np.stack([offs[16 * r : 16 * r + 16].T.reshape(-1) for r in range(8)]).astype(np.int64)
    return lists[np.arange(k) % 512 // 64]


def pack_weight(w):
    k, n = w.shape
    w = f64(np.asarray(w, np.float32).astype(ml_dtypes.bfloat16)).reshape(k // 32, 32, n)
    amax = np.abs(w).max(1)
    byte = np.clip(np.where(amax > 0, np.frexp(amax)[1] - 1 + 127 - 7, 1), 1, 254)
    scaled = (w * np.exp2(127.0 - byte)[:, None, :]).reshape(k, n).astype(np.float32)
    words = np.ascontiguousarray(scaled.reshape(k // 512, 128, 4, n).transpose(0, 1, 3, 2)).astype(ml_dtypes.float8_e4m3fn).view(np.uint8)
    return words, np.ascontiguousarray(byte.astype(np.uint8).reshape(k // 512, 16, n))


def unpack_weight(words, scales):
    g, p, n, _ = words.shape
    vals = np.ascontiguousarray(words).view(ml_dtypes.float8_e4m3fn).astype(np.float64) * np.repeat(np.exp2(scales.astype(np.float64) - 127.0), 8, axis=1)[..., None]
    return vals.transpose(0, 1, 3, 2).reshape(g * 512, n)


def sigmoid(v):
    return 1.0 / (1.0 + np.exp(-np.maximum(v, -700.0)))


K, T, S, H, C = 512, 2048, 512, 512, 512


def setup_inputs():
    n = np.random.standard_normal
    s = mx_kscale(K)[:, None]
    packed_xT = pack_weight(n((K, T)) * s)
    return {
        "x_words": packed_xT[0],
        "x_scales": packed_xT[1],
        "w1": (n((K, H)) / np.sqrt(K) / s).astype(np.float32),
        "gs": (np.random.uniform(0.5, 1.5, (K, 1)) / s).astype(np.float32),
        "offs": striped(np.random.permutation(T)[:S]),
        "n1": striped8(np.stack([np.random.permutation(S) for _ in range(8)])),
        "n2": striped8(np.stack([np.random.permutation(S) for _ in range(8)])),
        "ca": striped(np.random.permutation(T)[:C]),
        "hc": striped8(np.random.randint(0, T, (8, C))),
        "n3": striped8(np.stack([np.random.permutation(S) for _ in range(8)])),
        "n4": striped8(np.stack([np.random.permutation(S) for _ in range(8)])),
    }


def reference(x_words, x_scales, w1, gs, offs, n1, n2, ca, hc, n3, n4):
    x_ca = unpack_weight(x_words, x_scales)[:, unstriped(ca)]
    xq = unpack_weight(x_words, x_scales)[:, unstriped(offs)]
    y = mxq(f64(w1), 0, "e4m3").T @ xq
    pa = y[np.arange(H)[:, None], runs(n1, H)]
    pb = y[np.arange(H)[:, None], runs(n2, H)]
    z = f64(gs) * (np.maximum(np.maximum(y, pa), pb) - (0.5 * (np.minimum(np.minimum(y, pa), pb))))
    zq = mxq(z, 0, "e4m3")
    a = 0.0625 * (x_ca.T @ zq)
    x_hc = unpack_weight(x_words, x_scales)[np.arange(K)[:, None], runs(hc, K)]
    b = 0.0625 * (x_hc.T @ zq)
    return a * (sigmoid(b[np.arange(C)[:, None], runs(n4, C)])) - (0.5 * (a[np.arange(C)[:, None], runs(n3, C)]))

@@ -1,0 +1,171 @@
+from contextlib import ExitStack
+
+import concourse.mybir as mybir
+
+K, T, S, H, C = 512, 2048, 512, 512, 512
+FLOPS = 2 * K * (H * S + 2 * C * S)
+
+F32 = mybir.dt.float32
+BF16 = mybir.dt.bfloat16
+I32 = mybir.dt.int32
+U32 = mybir.dt.uint32
+U16 = mybir.dt.uint16
+U8 = mybir.dt.uint8
+FP8X4 = mybir.dt.float8_e4m3fn_x4
+ALU = mybir.AluOpType
+ACT = mybir.ActivationFunctionType
+
+P = 128
+PACK = 4
+TILES = 4
+HALF = 256
+LCOLS = HALF // 16
+
+
+def tile_picked_cdhgatebrange_none_p_kernel(tc, x_words, x_scales, w1, gs, offs, n1, n2, ca, hc, n3, n4, out):
+    nc = tc.nc
+    with ExitStack() as ctx:
+        keep = ctx.enter_context(tc.tile_pool(name="keep", bufs=1))
+        share = ctx.enter_context(tc.tile_pool(name="share", bufs=1))
+        psum = ctx.enter_context(tc.psum_pool(name="psum", bufs=1))
+
+        def new(name, shape, dtype):
+            return keep.tile(shape, dtype, name=name, align_bytes=64)
+
+        def load_list(name, src):
+            t = new(name, [P, S // 16], U16)
+            nc.sync.dma_start(t[:], src)
+            return t
+
+        xs = new("xs", [P, T], U8)
+        nc.vector.memset(xs[:].bitcast(I32), 0)
+        l_offs = load_list("l_offs", offs)
+        l_hc = load_list("l_hc", hc)
+        xs_i = xs[:].bitcast(I32)
+        rows = x_scales[0].bitcast(I32)
+        nc.sync.dma_start(xs_i[0:P:16, :], rows[0:16:2, :])
+        nc.sync.dma_start(xs_i[1:P:16, :], rows[1:16:2, :])
+        nc.sync.dma_start(xs_i[2:P:32, :], rows[2:16:4, :])
+        nc.sync.dma_start(xs_i[3:P:32, :], rows[3:16:4, :])
+        w_raw = new("w_raw", [P, PACK, H], F32)
+        nc.sync.dma_start(w_raw[:], w1.rearrange("(p j) c -> p j c", j=PACK))
+        xw = new("xw", [P, T], U32)
+        nc.sync.dma_start(xw[:].bitcast(I32), x_words[0].rearrange("p n t -> p (n t)").bitcast(I32))
+        l_ca = load_list("l_ca", ca)
+        l_n1 = load_list("l_n1", n1)
+        l_n2 = load_list("l_n2", n2)
+        g4 = new("g4", [P, TILES], F32)
+        nc.sync.dma_start(g4[:], gs.rearrange("(p t) o -> p (t o)", t=TILES))
+        l_n3 = load_list("l_n3", n3)
+        l_n4 = load_list("l_n4", n4)
+
+        def dealt(ap):
+            return ap.rearrange("p (t g q) -> p g t q", t=TILES, q=16)
+
+        q_s = new("q_s", [P, S], U8)
+        nc.vector.tensor_copy(q_s[:], xs[:].indirect(l_offs[:]))
+        hc_s0 = new("hc_s0", [P, C], U8)
+        nc.vector.tensor_copy(hc_s0[:], xs[:].indirect(l_hc[:]))
+        hc_s = new("hc_s", [P, C], U8)
+        hc_si = hc_s[:].bitcast(I32)
+        nc.vector.tensor_copy(
+            hc_si.rearrange("p (t g q) -> p g t q", t=TILES, q=4),
+            hc_s0[:].bitcast(I32).rearrange("p (g t q) -> p g t q", t=TILES, q=4),
+        )
+        nc.sync.dma_start(hc_si[2:P:32, :], hc_si[16:P:32, :])
+        nc.sync.dma_start(hc_si[3:P:32, :], hc_si[17:P:32, :])
+
+        w_bf = share.tile([P, TILES, P, PACK], BF16, name="w_bf", align_bytes=64, offset=0)
+        nc.scalar.copy(
+            w_bf[:].rearrange("p t m j -> p m j t"),
+            w_raw[:].rearrange("p j (m t) -> p m j t", t=TILES),
+        )
+        w_c = new("w_c", [P, H], U32)
+        w_s = new("w_s", [P, H], U8)
+        nc.vector.quantize_mx(out=w_c[:].bitcast(FP8X4), scales=w_s[:], in_=w_bf[:].rearrange("p t m j -> p (t m j)"))
+
+        q_w = new("q_w", [P, S], U32)
+        nc.vector.tensor_copy(q_w[:], xw[:].indirect(l_offs[:]))
+
+        banks = [psum.tile([P, 512], F32, name="bank%d" % i) for i in range(8)]
+        y = [new("y%d" % t, [P, S], F32) for t in range(TILES)]
+        for t in range(TILES):
+            cols = slice(P * t, P * (t + 1))
+            nc.tensor.matmul_mx(out=banks[4 + t][:], lhsT=w_c[:, cols].bitcast(FP8X4), lhsT_scale=w_s[:, cols],
+                                rhs=q_w[:].bitcast(FP8X4), rhs_scale=q_s[:], start=True, stop=True)
+
+        ca_s = share.tile([P, C], U8, name="ca_s", align_bytes=64, offset=2048)
+        nc.vector.tensor_copy(dealt(ca_s[:]), xs[:].indirect(l_ca[:]))
+        ca_w = share.tile([P, C], U32, name="ca_w", align_bytes=64, offset=0)
+        nc.vector.tensor_copy(dealt(ca_w[:]), xw[:].indirect(l_ca[:]))
+        hc_w0 = share.tile([P, C], U32, name="hc_w0", align_bytes=64, offset=2560)
+        nc.vector.tensor_copy(hc_w0[:], xw[:].indirect(l_hc[:]))
+        hc_w = new("hc_w", [P, C], U32)
+        nc.vector.tensor_copy(dealt(hc_w[:]), hc_w0[:].rearrange("p (g t q) -> p g t q", t=TILES, q=16))
+
+        sg = [new("sg%d" % t, [P, S], F32) for t in range(TILES)]
+        ah = [new("ah%d" % t, [P, S], F32) for t in range(TILES)]
+
+        def leave(h):
+            js = slice(HALF * h, HALF * (h + 1))
+            for t in range(TILES):
+                part = slice(HALF * (t % 2), HALF * (t % 2 + 1))
+                nc.scalar.activation(sg[t][:, js], banks[4 * h + 2 + t // 2][:, part], ACT.Sigmoid, scale=0.0625)
+                nc.scalar.activation(ah[t][:, js], banks[4 * h + t // 2][:, part], ACT.Copy, scale=-0.03125)
+
+        for h in range(2):
+            js = slice(HALF * h, HALF * (h + 1))
+            ls = slice(LCOLS * h, LCOLS * (h + 1))
+            zf = new("zf%d" % h, [P, TILES, HALF], F32)
+            for u in range(2):
+                pa = new("pa%d%d" % (h, u), [P, 2, HALF], F32)
+                pb = new("pb%d%d" % (h, u), [P, 2, HALF], F32)
+                hi = new("hi%d%d" % (h, u), [P, 2, HALF], F32)
+                lo = new("lo%d%d" % (h, u), [P, 2, HALF], F32)
+                hi2 = new("hj%d%d" % (h, u), [P, 2, HALF], F32)
+                lo2 = new("lp%d%d" % (h, u), [P, 2, HALF], F32)
+                r = new("r%d%d" % (h, u), [P, 2, HALF], F32)
+                for e in range(2):
+                    t = 2 * u + e
+                    if h == 0:
+                        nc.scalar.copy(y[t][:], banks[4 + t][:])
+                    nc.scalar.activation(pa[:, e, :], y[t][:].indirect(l_n1[:, ls]), ACT.Copy)
+                    nc.vector.tensor_tensor(hi[:, e, :], pa[:, e, :], y[t][:, js], ALU.max)
+                    nc.vector.tensor_tensor(lo[:, e, :], pa[:, e, :], y[t][:, js], ALU.min)
+                for e in range(2):
+                    t = 2 * u + e
+                    nc.scalar.activation(pb[:, e, :], y[t][:].indirect(l_n2[:, ls]), ACT.Copy)
+                nc.vector.tensor_tensor(hi2[:], hi[:], pb[:], ALU.max)
+                nc.vector.tensor_tensor(lo2[:], lo[:], pb[:], ALU.min)
+                nc.vector.scalar_tensor_tensor(r[:], lo2[:], -0.5, hi2[:], ALU.mult, ALU.add)
+                for e in range(2):
+                    t = 2 * u + e
+                    nc.vector.tensor_scalar(zf[:, t, :], r[:, e, :], g4[:, t : t + 1], None, ALU.mult)
+            zb = new("zb%d" % h, [P, HALF, PACK], BF16)
+            nc.vector.tensor_copy(
+                zb[:].rearrange("p (c i) t -> p c t i", i=4),
+                zf[:].rearrange("p t (c i) -> p c t i", i=4),
+            )
+            z_c = new("z_c%d" % h, [P, HALF], U32)
+            z_s = new("z_s%d" % h, [P, HALF], U8)
+            nc.vector.quantize_mx(out=z_c[:].bitcast(FP8X4), scales=z_s[:], in_=zb[:].rearrange("p c t -> p (c t)"))
+            for t in range(TILES):
+                cols = slice(P * t, P * (t + 1))
+                part = slice(HALF * (t % 2), HALF * (t % 2 + 1))
+                for words, planes, bank in ((hc_w, hc_s, banks[4 * h + 2 + t // 2]), (ca_w, ca_s, banks[4 * h + t // 2])):
+                    nc.tensor.matmul_mx(out=bank[:, part], lhsT=words[:, cols].bitcast(FP8X4), lhsT_scale=planes[:, cols],
+                                        rhs=z_c[:].bitcast(FP8X4), rhs_scale=z_s[:], start=True, stop=True)
+            leave(h)
+
+        out_rows = out.rearrange("(g t q) j -> t g q j", t=TILES, q=16)
+        for t in range(TILES):
+            for h in range(2):
+                js = slice(HALF * h, HALF * (h + 1))
+                ls = slice(LCOLS * h, LCOLS * (h + 1))
+                prod = new("prod%d%d" % (t, h), [P, HALF], F32)
+                far = new("far%d%d" % (t, h), [P, HALF], F32)
+                res = new("res%d%d" % (t, h), [P, HALF], F32)
+                nc.vector.tensor_tensor(prod[:], sg[t][:].indirect(l_n4[:, ls]), ah[t][:, js], ALU.mult)
+                nc.scalar.activation(far[:], ah[t][:].indirect(l_n3[:, ls]), ACT.Copy)
+                nc.vector.scalar_tensor_tensor(res[:], prod[:], -2.0, far[:], ALU.mult, ALU.add)
+                nc.sync.dma_start(out_rows[t][:, :, js], res[:])

@@ -41,14 +41,16 @@ def tile_picked_cdhgatebrange_none_p_kernel(tc, x_words, x_scales, w1, gs, offs,
         nc.vector.memset(xs[:].bitcast(I32), 0)
         l_offs = load_list("l_offs", offs)
         l_hc = load_list("l_hc", hc)
+        w_rows = w1.rearrange("(p j) c -> p j c", j=PACK)
+        w_raw = [new("w_raw%d" % h, [P, PACK, H // 2], F32) for h in range(2)]
+        nc.sync.dma_start(w_raw[0][:], w_rows[:, :, 0 : H // 2])
         xs_i = xs[:].bitcast(I32)
         rows = x_scales[0].bitcast(I32)
         nc.sync.dma_start(xs_i[0:P:16, :], rows[0:16:2, :])
         nc.sync.dma_start(xs_i[1:P:16, :], rows[1:16:2, :])
         nc.sync.dma_start(xs_i[2:P:32, :], rows[2:16:4, :])
         nc.sync.dma_start(xs_i[3:P:32, :], rows[3:16:4, :])
-        w_raw = new("w_raw", [P, PACK, H], F32)
-        nc.sync.dma_start(w_raw[:], w1.rearrange("(p j) c -> p j c", j=PACK))
+        nc.sync.dma_start(w_raw[1][:], w_rows[:, :, H // 2 : H])
         xw = new("xw", [P, T], U32)
         nc.sync.dma_start(xw[:].bitcast(I32), x_words[0].rearrange("p n t -> p (n t)").bitcast(I32))
         l_ca = load_list("l_ca", ca)
@@ -76,23 +78,27 @@ def tile_picked_cdhgatebrange_none_p_kernel(tc, x_words, x_scales, w1, gs, offs,
         nc.sync.dma_start(hc_si[3:P:32, :], hc_si[17:P:32, :])
 
         w_bf = share.tile([P, TILES, P, PACK], BF16, name="w_bf", align_bytes=64, offset=0)
-        nc.scalar.copy(
-            w_bf[:].rearrange("p t m j -> p m j t"),
-            w_raw[:].rearrange("p j (m t) -> p m j t", t=TILES),
-        )
+        for h in range(2):
+            nc.scalar.copy(
+                w_bf[:, :, 64 * h : 64 * (h + 1), :].rearrange("p t m j -> p m j t"),
+                w_raw[h][:].rearrange("p j (m t) -> p m j t", t=TILES),
+            )
         w_c = new("w_c", [P, H], U32)
         w_s = new("w_s", [P, H], U8)
         nc.vector.quantize_mx(out=w_c[:].bitcast(FP8X4), scales=w_s[:], in_=w_bf[:].rearrange("p t m j -> p (t m j)"))
 
         q_w = new("q_w", [P, S], U32)
-        nc.vector.tensor_copy(q_w[:], xw[:].indirect(l_offs[:]))
+        for h in range(2):
+            nc.vector.tensor_copy(q_w[:, HALF * h : HALF * (h + 1)], xw[:].indirect(l_offs[:, LCOLS * h : LCOLS * (h + 1)]))
 
         banks = [psum.tile([P, 512], F32, name="bank%d" % i) for i in range(8)]
         y = [new("y%d" % t, [P, S], F32) for t in range(TILES)]
         for t in range(TILES):
             cols = slice(P * t, P * (t + 1))
-            nc.tensor.matmul_mx(out=banks[4 + t][:], lhsT=w_c[:, cols].bitcast(FP8X4), lhsT_scale=w_s[:, cols],
-                                rhs=q_w[:].bitcast(FP8X4), rhs_scale=q_s[:], start=True, stop=True)
+            for h in range(2):
+                js = slice(HALF * h, HALF * (h + 1))
+                nc.tensor.matmul_mx(out=banks[4 + t][:, js], lhsT=w_c[:, cols].bitcast(FP8X4), lhsT_scale=w_s[:, cols],
+                                    rhs=q_w[:, js].bitcast(FP8X4), rhs_scale=q_s[:, js], start=True, stop=True)
 
         ca_s = share.tile([P, C], U8, name="ca_s", align_bytes=64, offset=2048)
         nc.vector.tensor_copy(dealt(ca_s[:]), xs[:].indirect(l_ca[:]))
@@ -101,71 +107,97 @@ def tile_picked_cdhgatebrange_none_p_kernel(tc, x_words, x_scales, w1, gs, offs,
         hc_w0 = share.tile([P, C], U32, name="hc_w0", align_bytes=64, offset=2560)
         nc.vector.tensor_copy(hc_w0[:], xw[:].indirect(l_hc[:]))
         hc_w = new("hc_w", [P, C], U32)
-        nc.vector.tensor_copy(dealt(hc_w[:]), hc_w0[:].rearrange("p (g t q) -> p g t q", t=TILES, q=16))
+        for t in range(TILES):
+            nc.sync.dma_start(
+                hc_w[:, P * t : P * (t + 1)].bitcast(I32).rearrange("p (g q) -> p g q", q=16),
+                hc_w0[:].bitcast(I32).rearrange("p (g t q) -> p t g q", t=TILES, q=16)[:, t],
+            )
 
         sg = [new("sg%d" % t, [P, S], F32) for t in range(TILES)]
         ah = [new("ah%d" % t, [P, S], F32) for t in range(TILES)]
 
-        def leave(h):
-            js = slice(HALF * h, HALF * (h + 1))
-            for t in range(TILES):
-                part = slice(HALF * (t % 2), HALF * (t % 2 + 1))
-                nc.scalar.activation(sg[t][:, js], banks[4 * h + 2 + t // 2][:, part], ACT.Sigmoid, scale=0.0625)
-                nc.scalar.activation(ah[t][:, js], banks[4 * h + t // 2][:, part], ACT.Copy, scale=-0.03125)
+        CH = [(0, 256, 1), (256, 384, 2), (384, 512, 2)]
 
-        for h in range(2):
-            js = slice(HALF * h, HALF * (h + 1))
-            ls = slice(LCOLS * h, LCOLS * (h + 1))
-            zf = new("zf%d" % h, [P, TILES, HALF], F32)
-            for u in range(2):
-                pa = new("pa%d%d" % (h, u), [P, 2, HALF], F32)
-                pb = new("pb%d%d" % (h, u), [P, 2, HALF], F32)
-                hi = new("hi%d%d" % (h, u), [P, 2, HALF], F32)
-                lo = new("lo%d%d" % (h, u), [P, 2, HALF], F32)
-                hi2 = new("hj%d%d" % (h, u), [P, 2, HALF], F32)
-                lo2 = new("lp%d%d" % (h, u), [P, 2, HALF], F32)
-                r = new("r%d%d" % (h, u), [P, 2, HALF], F32)
-                for e in range(2):
-                    t = 2 * u + e
+        EV = {0: 0, 1: 256}
+        VEV = ()
+
+        def pieces(a, b):
+            res = []
+            while a < b:
+                n = 256 if b - a >= 256 else 128
+                res.append((a, a + n))
+                a = a + n
+            return res
+
+        def a_bank(t):
+            return banks[2 * t + 1]
+
+        def b_bank(t):
+            return banks[2 * t]
+
+        def leave(t, a, b):
+            nc.scalar.activation(sg[t][:, a:b], b_bank(t)[:, a:b], ACT.Sigmoid, scale=0.0625)
+            if b == S and t in VEV:
+                nc.vector.tensor_scalar(ah[t][:, a:b], a_bank(t)[:, a:b], -0.03125, None, ALU.mult)
+            else:
+                nc.scalar.activation(ah[t][:, a:b], a_bank(t)[:, a:b], ACT.Copy, scale=-0.03125)
+
+        def fetch(dst, t, lst, a, b):
+            for c, d in pieces(a, b):
+                nc.scalar.activation(dst[:, c - a : d - a], y[t][:].indirect(lst[:, c // 16 : d // 16]), ACT.Copy)
+
+        for h, (a, b, grp) in enumerate(CH):
+            w = b - a
+            zf = new("zf%d" % h, [P, TILES, w], F32)
+            for u in range(TILES // grp):
+                pa, pb, hi, lo, hi2, lo2, r = [new("%s%d%d" % (nm, h, u), [P, grp, w], F32) for nm in ("pa", "pb", "hi", "lo", "hj", "lp", "r")]
+                for e in range(grp):
+                    t = grp * u + e
                     if h == 0:
                         nc.scalar.copy(y[t][:], banks[4 + t][:])
-                    nc.scalar.activation(pa[:, e, :], y[t][:].indirect(l_n1[:, ls]), ACT.Copy)
-                    nc.vector.tensor_tensor(hi[:, e, :], pa[:, e, :], y[t][:, js], ALU.max)
-                    nc.vector.tensor_tensor(lo[:, e, :], pa[:, e, :], y[t][:, js], ALU.min)
-                for e in range(2):
-                    t = 2 * u + e
-                    nc.scalar.activation(pb[:, e, :], y[t][:].indirect(l_n2[:, ls]), ACT.Copy)
+                    fetch(pa[:, e, :], t, l_n1, a, b)
+                    nc.vector.tensor_tensor(hi[:, e, :], pa[:, e, :], y[t][:, a:b], ALU.max)
+                    nc.vector.tensor_tensor(lo[:, e, :], pa[:, e, :], y[t][:, a:b], ALU.min)
+                for e in range(grp):
+                    fetch(pb[:, e, :], grp * u + e, l_n2, a, b)
                 nc.vector.tensor_tensor(hi2[:], hi[:], pb[:], ALU.max)
                 nc.vector.tensor_tensor(lo2[:], lo[:], pb[:], ALU.min)
-                nc.vector.scalar_tensor_tensor(r[:], lo2[:], -0.5, hi2[:], ALU.mult, ALU.add)
-                for e in range(2):
-                    t = 2 * u + e
-                    nc.vector.tensor_scalar(zf[:, t, :], r[:, e, :], g4[:, t : t + 1], None, ALU.mult)
-            zb = new("zb%d" % h, [P, HALF, PACK], BF16)
-            nc.vector.tensor_copy(
+                nc.vector.scalar_tensor_tensor(zf[:, grp * u : grp * (u + 1), :], lo2[:], -0.5, hi2[:], ALU.mult, ALU.add)
+            zb = new("zb%d" % h, [P, w, PACK], BF16)
+            nc.vector.tensor_tensor(
                 zb[:].rearrange("p (c i) t -> p c t i", i=4),
                 zf[:].rearrange("p t (c i) -> p c t i", i=4),
+                g4[:].unsqueeze(1).unsqueeze(3).to_broadcast([P, w // 4, TILES, 4]),
+                ALU.mult,
             )
-            z_c = new("z_c%d" % h, [P, HALF], U32)
-            z_s = new("z_s%d" % h, [P, HALF], U8)
+            z_c = new("z_c%d" % h, [P, w], U32)
+            z_s = new("z_s%d" % h, [P, w], U8)
             nc.vector.quantize_mx(out=z_c[:].bitcast(FP8X4), scales=z_s[:], in_=zb[:].rearrange("p c t -> p (c t)"))
             for t in range(TILES):
                 cols = slice(P * t, P * (t + 1))
-                part = slice(HALF * (t % 2), HALF * (t % 2 + 1))
-                for words, planes, bank in ((hc_w, hc_s, banks[4 * h + 2 + t // 2]), (ca_w, ca_s, banks[4 * h + t // 2])):
-                    nc.tensor.matmul_mx(out=bank[:, part], lhsT=words[:, cols].bitcast(FP8X4), lhsT_scale=planes[:, cols],
-                                        rhs=z_c[:].bitcast(FP8X4), rhs_scale=z_s[:], start=True, stop=True)
-            leave(h)
+                for words, planes, bank in ((hc_w, hc_s, b_bank(t)), (ca_w, ca_s, a_bank(t))):
+                    for c, d in pieces(a, b):
+                        nc.tensor.matmul_mx(out=bank[:, c:d], lhsT=words[:, cols].bitcast(FP8X4), lhsT_scale=planes[:, cols],
+                                            rhs=z_c[:, c - a : d - a].bitcast(FP8X4), rhs_scale=z_s[:, c - a : d - a], start=True, stop=True)
+            if h in EV:
+                for t in range(TILES):
+                    leave(t, EV[h], b)
 
         out_rows = out.rearrange("(g t q) j -> t g q j", t=TILES, q=16)
         for t in range(TILES):
-            for h in range(2):
-                js = slice(HALF * h, HALF * (h + 1))
-                ls = slice(LCOLS * h, LCOLS * (h + 1))
-                prod = new("prod%d%d" % (t, h), [P, HALF], F32)
-                far = new("far%d%d" % (t, h), [P, HALF], F32)
-                res = new("res%d%d" % (t, h), [P, HALF], F32)
-                nc.vector.tensor_tensor(prod[:], sg[t][:].indirect(l_n4[:, ls]), ah[t][:, js], ALU.mult)
+            leave(t, CH[-1][0], CH[-1][1])
+            for h, (c, d) in enumerate([(0, 256), (256, 384), (384, 512)] if t == TILES - 1 else [(0, 256), (256, 512)]):
+                js = slice(c, d)
+                ls = slice(c // 16, d // 16)
+                prod = new("prod%d%d" % (t, h), [P, d - c], F32)
+                far = new("far%d%d" % (t, h), [P, d - c], F32)
+                res = new("res%d%d" % (t, h), [P, d - c], F32)
+                if (t, h) in ():
+                    near = new("near%d%d" % (t, h), [P, d - c], F32)
+                    nc.scalar.activation(near[:], sg[t][:].indirect(l_n4[:, ls]), ACT.Copy)
+                    nc.vector.tensor_tensor(prod[:], near[:], ah[t][:, js], ALU.mult)
+                else:
+                    nc.vector.tensor_tensor(prod[:], sg[t][:].indirect(l_n4[:, ls]), ah[t][:, js], ALU.mult)
                 nc.scalar.activation(far[:], ah[t][:].indirect(l_n3[:, ls]), ACT.Copy)
                 nc.vector.scalar_tensor_tensor(res[:], prod[:], -2.0, far[:], ALU.mult, ALU.add)
                 nc.sync.dma_start(out_rows[t][:, :, js], res[:])

@@ -80,8 +80,8 @@ def tile_picked_cdhgatebrange_none_p_kernel(tc, x_words, x_scales, w1, gs, offs,
         w_bf = share.tile([P, TILES, P, PACK], BF16, name="w_bf", align_bytes=64, offset=0)
         for h in range(2):
             nc.scalar.copy(
-                w_bf[:, :, 64 * h : 64 * (h + 1), :].rearrange("p t m j -> p m j t"),
-                w_raw[h][:].rearrange("p j (m t) -> p m j t", t=TILES),
+                w_bf[:, :, 64 * h : 64 * (h + 1), :].rearrange("p t m j -> p m t j"),
+                w_raw[h][:].rearrange("p j (m t) -> p m t j", t=TILES),
             )
         w_c = new("w_c", [P, H], U32)
         w_s = new("w_s", [P, H], U8)
@@ -93,26 +93,18 @@ def tile_picked_cdhgatebrange_none_p_kernel(tc, x_words, x_scales, w1, gs, offs,
 
         banks = [psum.tile([P, 512], F32, name="bank%d" % i) for i in range(8)]
         y = [new("y%d" % t, [P, S], F32) for t in range(TILES)]
-        for t in range(TILES):
-            cols = slice(P * t, P * (t + 1))
+        for u in range(2):
             for h in range(2):
-                js = slice(HALF * h, HALF * (h + 1))
-                nc.tensor.matmul_mx(out=banks[4 + t][:, js], lhsT=w_c[:, cols].bitcast(FP8X4), lhsT_scale=w_s[:, cols],
-                                    rhs=q_w[:, js].bitcast(FP8X4), rhs_scale=q_s[:, js], start=True, stop=True)
+                for t in (2 * u, 2 * u + 1):
+                    cols = slice(P * t, P * (t + 1))
+                    js = slice(HALF * h, HALF * (h + 1))
+                    nc.tensor.matmul_mx(out=banks[4 * h + t][:, 0:HALF], lhsT=w_c[:, cols].bitcast(FP8X4), lhsT_scale=w_s[:, cols],
+                                        rhs=q_w[:, js].bitcast(FP8X4), rhs_scale=q_s[:, js], start=True, stop=True)
 
         ca_s = share.tile([P, C], U8, name="ca_s", align_bytes=64, offset=2048)
         nc.vector.tensor_copy(dealt(ca_s[:]), xs[:].indirect(l_ca[:]))
         ca_w = share.tile([P, C], U32, name="ca_w", align_bytes=64, offset=0)
         nc.vector.tensor_copy(dealt(ca_w[:]), xw[:].indirect(l_ca[:]))
-        hc_w0 = share.tile([P, C], U32, name="hc_w0", align_bytes=64, offset=2560)
-        nc.vector.tensor_copy(hc_w0[:], xw[:].indirect(l_hc[:]))
-        hc_w = new("hc_w", [P, C], U32)
-        for t in range(TILES):
-            nc.sync.dma_start(
-                hc_w[:, P * t : P * (t + 1)].bitcast(I32).rearrange("p (g q) -> p g q", q=16),
-                hc_w0[:].bitcast(I32).rearrange("p (g t q) -> p t g q", t=TILES, q=16)[:, t],
-            )
-
         sg = [new("sg%d" % t, [P, S], F32) for t in range(TILES)]
         ah = [new("ah%d" % t, [P, S], F32) for t in range(TILES)]
 
@@ -146,46 +138,108 @@ def tile_picked_cdhgatebrange_none_p_kernel(tc, x_words, x_scales, w1, gs, offs,
             for c, d in pieces(a, b):
                 nc.scalar.activation(dst[:, c - a : d - a], y[t][:].indirect(lst[:, c // 16 : d // 16]), ACT.Copy)
 
-        for h, (a, b, grp) in enumerate(CH):
+        def held(name, shape, dtype, place):
+            return share.tile(shape, dtype, name=name, align_bytes=64, offset=8192 + 4096 * place)
+
+        hc_w = new("hc_w", [P, C], U32)
+
+        def hashed_words(place):
+            hc_w0 = held("hc_w0", [P, C], U32, place) if place >= 0 else share.tile([P, C], U32, name="hc_w0", align_bytes=64, offset=2560)
+            nc.vector.tensor_copy(hc_w0[:], xw[:].indirect(l_hc[:]))
+            for v in range(TILES):
+                nc.sync.dma_start(
+                    hc_w[:, P * v : P * (v + 1)].bitcast(I32).rearrange("p (g q) -> p g q", q=16),
+                    hc_w0[:].bitcast(I32).rearrange("p (g t q) -> p t g q", t=TILES, q=16)[:, v],
+                )
+
+        EARLY = 3
+        z_c = new("z_c", [P, S], U32)
+        z_s = new("z_s", [P, S], U8)
+
+        def finish(h, zf, a, b, scaled, zb=None):
             w = b - a
-            zf = new("zf%d" % h, [P, TILES, w], F32)
-            for u in range(TILES // grp):
-                pa, pb, hi, lo, hi2, lo2, r = [new("%s%d%d" % (nm, h, u), [P, grp, w], F32) for nm in ("pa", "pb", "hi", "lo", "hj", "lp", "r")]
-                for e in range(grp):
-                    t = grp * u + e
-                    if h == 0:
-                        nc.scalar.copy(y[t][:], banks[4 + t][:])
-                    fetch(pa[:, e, :], t, l_n1, a, b)
-                    nc.vector.tensor_tensor(hi[:, e, :], pa[:, e, :], y[t][:, a:b], ALU.max)
-                    nc.vector.tensor_tensor(lo[:, e, :], pa[:, e, :], y[t][:, a:b], ALU.min)
-                for e in range(grp):
-                    fetch(pb[:, e, :], grp * u + e, l_n2, a, b)
-                nc.vector.tensor_tensor(hi2[:], hi[:], pb[:], ALU.max)
-                nc.vector.tensor_tensor(lo2[:], lo[:], pb[:], ALU.min)
-                nc.vector.scalar_tensor_tensor(zf[:, grp * u : grp * (u + 1), :], lo2[:], -0.5, hi2[:], ALU.mult, ALU.add)
-            zb = new("zb%d" % h, [P, w, PACK], BF16)
-            nc.vector.tensor_tensor(
-                zb[:].rearrange("p (c i) t -> p c t i", i=4),
-                zf[:].rearrange("p t (c i) -> p c t i", i=4),
-                g4[:].unsqueeze(1).unsqueeze(3).to_broadcast([P, w // 4, TILES, 4]),
-                ALU.mult,
-            )
-            z_c = new("z_c%d" % h, [P, w], U32)
-            z_s = new("z_s%d" % h, [P, w], U8)
-            nc.vector.quantize_mx(out=z_c[:].bitcast(FP8X4), scales=z_s[:], in_=zb[:].rearrange("p c t -> p (c t)"))
+            if zb is None:
+                zb = new("zb%d" % h, [P, w, PACK], BF16)
+            if scaled:
+                nc.vector.tensor_copy(zb[:].rearrange("p (c i) t -> p c t i", i=4), zf.rearrange("p t (c i) -> p c t i", i=4))
+            else:
+                nc.vector.tensor_tensor(
+                    zb[:].rearrange("p (c i) t -> p c t i", i=4),
+                    zf.rearrange("p t (c i) -> p c t i", i=4),
+                    g4[:].unsqueeze(1).unsqueeze(3).to_broadcast([P, w // 4, TILES, 4]),
+                    ALU.mult,
+                )
+            nc.vector.quantize_mx(out=z_c[:, a:b].bitcast(FP8X4), scales=z_s[:, a:b], in_=zb[:].rearrange("p c t -> p (c t)"))
             for t in range(TILES):
+                if h == 1 and t >= EARLY:
+                    continue
+                lo_col = HALF if h == 2 and t >= EARLY else a
                 cols = slice(P * t, P * (t + 1))
                 for words, planes, bank in ((hc_w, hc_s, b_bank(t)), (ca_w, ca_s, a_bank(t))):
-                    for c, d in pieces(a, b):
-                        nc.tensor.matmul_mx(out=bank[:, c:d], lhsT=words[:, cols].bitcast(FP8X4), lhsT_scale=planes[:, cols],
-                                            rhs=z_c[:, c - a : d - a].bitcast(FP8X4), rhs_scale=z_s[:, c - a : d - a], start=True, stop=True)
-            if h in EV:
-                for t in range(TILES):
-                    leave(t, EV[h], b)
+                    nc.tensor.matmul_mx(out=bank[:, lo_col:b], lhsT=words[:, cols].bitcast(FP8X4), lhsT_scale=planes[:, cols],
+                                        rhs=z_c[:, lo_col:b].bitcast(FP8X4), rhs_scale=z_s[:, lo_col:b], start=True, stop=True)
+            if b < S:
+                for t in range(TILES if h == 0 else EARLY):
+                    leave(t, a, b)
+
+        HCL = -1
+        SCA = False
+        if HCL < 0:
+            hashed_words(-1)
+        if SCA:
+            gn = new("gn", [P, TILES], F32)
+            nc.scalar.activation(gn[:], g4[:], ACT.Copy, scale=-0.5)
+        for t in range(TILES):
+            for v in range(2):
+                nc.scalar.copy(y[t][:, HALF * v : HALF * (v + 1)], banks[4 * v + t][:, 0:HALF])
+        zfa = new("zfa", [P, TILES, HALF], F32)
+        hja = held("hja", [P, TILES, HALF], F32, 1)
+        lpa = new("lpa", [P, TILES, HALF], F32)
+        for t in range(TILES):
+            pa, pb, hi, lo = [new("%sa%d" % (nm, t), [P, HALF], F32) for nm in ("pa", "pb", "hi", "lo")]
+            if t == HCL:
+                hi = held("hi_held", [P, HALF], F32, 0)
+            fetch(pa, t, l_n1, 0, HALF)
+            nc.vector.tensor_tensor(hi[:], pa[:], y[t][:, 0:HALF], ALU.max)
+            nc.vector.tensor_tensor(lo[:], pa[:], y[t][:, 0:HALF], ALU.min)
+            fetch(pb, t, l_n2, 0, HALF)
+            nc.vector.tensor_tensor(hja[:, t, :], hi[:], pb[:], ALU.max)
+            nc.vector.tensor_tensor(lpa[:, t, :], lo[:], pb[:], ALU.min)
+            if t == HCL:
+                hashed_words(0)
+            if not SCA:
+                nc.vector.scalar_tensor_tensor(zfa[:, t, :], lpa[:, t, :], -0.5, hja[:, t, :], ALU.mult, ALU.add)
+        if not SCA:
+            finish(0, zfa[:], 0, HALF, False)
+        pa, hi, lo = [new("%sb" % nm, [P, TILES, HALF], F32) for nm in ("pa", "hi", "lo")]
+        for t in range(TILES):
+            fetch(pa[:, t, :], t, l_n1, HALF, S)
+            nc.vector.tensor_tensor(hi[:, t, :], pa[:, t, :], y[t][:, HALF:S], ALU.max)
+            nc.vector.tensor_tensor(lo[:, t, :], pa[:, t, :], y[t][:, HALF:S], ALU.min)
+        if SCA:
+            cha = new("cha", [P, TILES, HALF], F32)
+            for t in range(TILES):
+                nc.scalar.activation(cha[:, t, :], hja[:, t, :], ACT.Copy, scale=g4[:, t : t + 1])
+                nc.vector.scalar_tensor_tensor(zfa[:, t, :], lpa[:, t, :], gn[:, t : t + 1], cha[:, t, :], ALU.mult, ALU.add)
+            finish(0, zfa[:], 0, HALF, True)
+            pb = held("pbb", [P, TILES, HALF], F32, 1)
+        else:
+            pb = new("pbb", [P, TILES, HALF], F32)
+        for a, b in [(256, 384), (384, 512)]:
+            for t in range(TILES):
+                fetch(pb[:, t, a - HALF : b - HALF], t, l_n2, a, b)
+        for h, (a, b) in enumerate([(256, 384), (384, 512)]):
+            w = b - a
+            js = slice(a - HALF, b - HALF)
+            hj, lp, zf = [new("%sc%d" % (nm, h), [P, TILES, w], F32) for nm in ("hj", "lp", "zf")]
+            nc.vector.tensor_tensor(hj[:], hi[:, :, js], pb[:, :, js], ALU.max)
+            nc.vector.tensor_tensor(lp[:], lo[:, :, js], pb[:, :, js], ALU.min)
+            nc.vector.scalar_tensor_tensor(zf[:], lp[:], -0.5, hj[:], ALU.mult, ALU.add)
+            finish(h + 1, zf[:], a, b, False)
 
         out_rows = out.rearrange("(g t q) j -> t g q j", t=TILES, q=16)
         for t in range(TILES):
-            leave(t, CH[-1][0], CH[-1][1])
+            leave(t, 384 if t < EARLY else HALF, S)
             for h, (c, d) in enumerate([(0, 256), (256, 384), (384, 512)] if t == TILES - 1 else [(0, 256), (256, 512)]):
                 js = slice(c, d)
                 ls = slice(c // 16, d // 16)

from contextlib import ExitStack

import concourse.mybir as mybir

K, T, S, H, C = 512, 2048, 512, 512, 512
FLOPS = 2 * K * (H * S + 2 * C * S)

F32 = mybir.dt.float32
BF16 = mybir.dt.bfloat16
I32 = mybir.dt.int32
U32 = mybir.dt.uint32
U16 = mybir.dt.uint16
U8 = mybir.dt.uint8
FP8X4 = mybir.dt.float8_e4m3fn_x4
ALU = mybir.AluOpType
ACT = mybir.ActivationFunctionType

P = 128
PACK = 4
TILES = 4
HALF = 256
LCOLS = HALF // 16


def tile_picked_cdhgatebrange_none_p_kernel(tc, x_words, x_scales, w1, gs, offs, n1, n2, ca, hc, n3, n4, out):
    nc = tc.nc
    with ExitStack() as ctx:
        keep = ctx.enter_context(tc.tile_pool(name="keep", bufs=1))
        share = ctx.enter_context(tc.tile_pool(name="share", bufs=1))
        psum = ctx.enter_context(tc.psum_pool(name="psum", bufs=1))

        def new(name, shape, dtype):
            return keep.tile(shape, dtype, name=name, align_bytes=64)

        def load_list(name, src):
            t = new(name, [P, S // 16], U16)
            nc.sync.dma_start(t[:], src)
            return t

        xs = new("xs", [P, T], U8)
        nc.vector.memset(xs[:].bitcast(I32), 0)
        l_offs = load_list("l_offs", offs)
        l_hc = load_list("l_hc", hc)
        w_rows = w1.rearrange("(p j) c -> p j c", j=PACK)
        w_raw = [new("w_raw%d" % h, [P, PACK, H // 2], F32) for h in range(2)]
        nc.sync.dma_start(w_raw[0][:], w_rows[:, :, 0 : H // 2])
        xs_i = xs[:].bitcast(I32)
        rows = x_scales[0].bitcast(I32)
        nc.sync.dma_start(xs_i[0:P:16, :], rows[0:16:2, :])
        nc.sync.dma_start(xs_i[1:P:16, :], rows[1:16:2, :])
        nc.sync.dma_start(xs_i[2:P:32, :], rows[2:16:4, :])
        nc.sync.dma_start(xs_i[3:P:32, :], rows[3:16:4, :])
        nc.sync.dma_start(w_raw[1][:], w_rows[:, :, H // 2 : H])
        xw = new("xw", [P, T], U32)
        nc.sync.dma_start(xw[:].bitcast(I32), x_words[0].rearrange("p n t -> p (n t)").bitcast(I32))
        l_ca = load_list("l_ca", ca)
        l_n1 = load_list("l_n1", n1)
        l_n2 = load_list("l_n2", n2)
        g4 = new("g4", [P, TILES], F32)
        nc.sync.dma_start(g4[:], gs.rearrange("(p t) o -> p (t o)", t=TILES))
        l_n3 = load_list("l_n3", n3)
        l_n4 = load_list("l_n4", n4)

        def dealt(ap):
            return ap.rearrange("p (t g q) -> p g t q", t=TILES, q=16)

        q_s = new("q_s", [P, S], U8)
        nc.vector.tensor_copy(q_s[:], xs[:].indirect(l_offs[:]))
        hc_s0 = new("hc_s0", [P, C], U8)
        nc.vector.tensor_copy(hc_s0[:], xs[:].indirect(l_hc[:]))
        hc_s = new("hc_s", [P, C], U8)
        hc_si = hc_s[:].bitcast(I32)
        nc.vector.tensor_copy(
            hc_si.rearrange("p (t g q) -> p g t q", t=TILES, q=4),
            hc_s0[:].bitcast(I32).rearrange("p (g t q) -> p g t q", t=TILES, q=4),
        )
        nc.sync.dma_start(hc_si[2:P:32, :], hc_si[16:P:32, :])
        nc.sync.dma_start(hc_si[3:P:32, :], hc_si[17:P:32, :])

        w_bf = share.tile([P, TILES, P, PACK], BF16, name="w_bf", align_bytes=64, offset=0)
        for h in range(2):
            nc.scalar.copy(
                w_bf[:, :, 64 * h : 64 * (h + 1), :].rearrange("p t m j -> p m t j"),
                w_raw[h][:].rearrange("p j (m t) -> p m t j", t=TILES),
            )
        w_c = new("w_c", [P, H], U32)
        w_s = new("w_s", [P, H], U8)
        nc.vector.quantize_mx(out=w_c[:].bitcast(FP8X4), scales=w_s[:], in_=w_bf[:].rearrange("p t m j -> p (t m j)"))

        q_w = new("q_w", [P, S], U32)
        for h in range(2):
            nc.vector.tensor_copy(q_w[:, HALF * h : HALF * (h + 1)], xw[:].indirect(l_offs[:, LCOLS * h : LCOLS * (h + 1)]))

        banks = [psum.tile([P, 512], F32, name="bank%d" % i) for i in range(8)]
        y = [new("y%d" % t, [P, S], F32) for t in range(TILES)]
        for u in range(2):
            for h in range(2):
                for t in (2 * u, 2 * u + 1):
                    cols = slice(P * t, P * (t + 1))
                    js = slice(HALF * h, HALF * (h + 1))
                    nc.tensor.matmul_mx(out=banks[4 * h + t][:, 0:HALF], lhsT=w_c[:, cols].bitcast(FP8X4), lhsT_scale=w_s[:, cols],
                                        rhs=q_w[:, js].bitcast(FP8X4), rhs_scale=q_s[:, js], start=True, stop=True)

        ca_s = share.tile([P, C], U8, name="ca_s", align_bytes=64, offset=2048)
        nc.vector.tensor_copy(dealt(ca_s[:]), xs[:].indirect(l_ca[:]))
        ca_w = share.tile([P, C], U32, name="ca_w", align_bytes=64, offset=0)
        nc.vector.tensor_copy(dealt(ca_w[:]), xw[:].indirect(l_ca[:]))
        sg = [new("sg%d" % t, [P, S], F32) for t in range(TILES)]
        ah = [new("ah%d" % t, [P, S], F32) for t in range(TILES)]

        CH = [(0, 256, 1), (256, 384, 2), (384, 512, 2)]

        EV = {0: 0, 1: 256}
        VEV = ()

        def pieces(a, b):
            res = []
            while a < b:
                n = 256 if b - a >= 256 else 128
                res.append((a, a + n))
                a = a + n
            return res

        def a_bank(t):
            return banks[2 * t + 1]

        def b_bank(t):
            return banks[2 * t]

        def leave(t, a, b):
            nc.scalar.activation(sg[t][:, a:b], b_bank(t)[:, a:b], ACT.Sigmoid, scale=0.0625)
            if b == S and t in VEV:
                nc.vector.tensor_scalar(ah[t][:, a:b], a_bank(t)[:, a:b], -0.03125, None, ALU.mult)
            else:
                nc.scalar.activation(ah[t][:, a:b], a_bank(t)[:, a:b], ACT.Copy, scale=-0.03125)

        def fetch(dst, t, lst, a, b):
            for c, d in pieces(a, b):
                nc.scalar.activation(dst[:, c - a : d - a], y[t][:].indirect(lst[:, c // 16 : d // 16]), ACT.Copy)

        def held(name, shape, dtype, place):
            return share.tile(shape, dtype, name=name, align_bytes=64, offset=8192 + 4096 * place)

        hc_w = new("hc_w", [P, C], U32)

        def hashed_words(place):
            hc_w0 = held("hc_w0", [P, C], U32, place) if place >= 0 else share.tile([P, C], U32, name="hc_w0", align_bytes=64, offset=2560)
            nc.vector.tensor_copy(hc_w0[:], xw[:].indirect(l_hc[:]))
            for v in range(TILES):
                nc.sync.dma_start(
                    hc_w[:, P * v : P * (v + 1)].bitcast(I32).rearrange("p (g q) -> p g q", q=16),
                    hc_w0[:].bitcast(I32).rearrange("p (g t q) -> p t g q", t=TILES, q=16)[:, v],
                )

        EARLY = 3
        z_c = new("z_c", [P, S], U32)
        z_s = new("z_s", [P, S], U8)

        def finish(h, zf, a, b, scaled, zb=None):
            w = b - a
            if zb is None:
                zb = new("zb%d" % h, [P, w, PACK], BF16)
            if scaled:
                nc.vector.tensor_copy(zb[:].rearrange("p (c i) t -> p c t i", i=4), zf.rearrange("p t (c i) -> p c t i", i=4))
            else:
                nc.vector.tensor_tensor(
                    zb[:].rearrange("p (c i) t -> p c t i", i=4),
                    zf.rearrange("p t (c i) -> p c t i", i=4),
                    g4[:].unsqueeze(1).unsqueeze(3).to_broadcast([P, w // 4, TILES, 4]),
                    ALU.mult,
                )
            nc.vector.quantize_mx(out=z_c[:, a:b].bitcast(FP8X4), scales=z_s[:, a:b], in_=zb[:].rearrange("p c t -> p (c t)"))
            for t in range(TILES):
                if h == 1 and t >= EARLY:
                    continue
                lo_col = HALF if h == 2 and t >= EARLY else a
                cols = slice(P * t, P * (t + 1))
                for words, planes, bank in ((hc_w, hc_s, b_bank(t)), (ca_w, ca_s, a_bank(t))):
                    nc.tensor.matmul_mx(out=bank[:, lo_col:b], lhsT=words[:, cols].bitcast(FP8X4), lhsT_scale=planes[:, cols],
                                        rhs=z_c[:, lo_col:b].bitcast(FP8X4), rhs_scale=z_s[:, lo_col:b], start=True, stop=True)
            if b < S:
                for t in range(TILES if h == 0 else EARLY):
                    leave(t, a, b)

        HCL = -1
        SCA = False
        if HCL < 0:
            hashed_words(-1)
        if SCA:
            gn = new("gn", [P, TILES], F32)
            nc.scalar.activation(gn[:], g4[:], ACT.Copy, scale=-0.5)
        for t in range(TILES):
            for v in range(2):
                nc.scalar.copy(y[t][:, HALF * v : HALF * (v + 1)], banks[4 * v + t][:, 0:HALF])
        zfa = new("zfa", [P, TILES, HALF], F32)
        hja = held("hja", [P, TILES, HALF], F32, 1)
        lpa = new("lpa", [P, TILES, HALF], F32)
        for t in range(TILES):
            pa, pb, hi, lo = [new("%sa%d" % (nm, t), [P, HALF], F32) for nm in ("pa", "pb", "hi", "lo")]
            if t == HCL:
                hi = held("hi_held", [P, HALF], F32, 0)
            fetch(pa, t, l_n1, 0, HALF)
            nc.vector.tensor_tensor(hi[:], pa[:], y[t][:, 0:HALF], ALU.max)
            nc.vector.tensor_tensor(lo[:], pa[:], y[t][:, 0:HALF], ALU.min)
            fetch(pb, t, l_n2, 0, HALF)
            nc.vector.tensor_tensor(hja[:, t, :], hi[:], pb[:], ALU.max)
            nc.vector.tensor_tensor(lpa[:, t, :], lo[:], pb[:], ALU.min)
            if t == HCL:
                hashed_words(0)
            if not SCA:
                nc.vector.scalar_tensor_tensor(zfa[:, t, :], lpa[:, t, :], -0.5, hja[:, t, :], ALU.mult, ALU.add)
        if not SCA:
            finish(0, zfa[:], 0, HALF, False)
        pa, hi, lo = [new("%sb" % nm, [P, TILES, HALF], F32) for nm in ("pa", "hi", "lo")]
        for t in range(TILES):
            fetch(pa[:, t, :], t, l_n1, HALF, S)
            nc.vector.tensor_tensor(hi[:, t, :], pa[:, t, :], y[t][:, HALF:S], ALU.max)
            nc.vector.tensor_tensor(lo[:, t, :], pa[:, t, :], y[t][:, HALF:S], ALU.min)
        if SCA:
            cha = new("cha", [P, TILES, HALF], F32)
            for t in range(TILES):
                nc.scalar.activation(cha[:, t, :], hja[:, t, :], ACT.Copy, scale=g4[:, t : t + 1])
                nc.vector.scalar_tensor_tensor(zfa[:, t, :], lpa[:, t, :], gn[:, t : t + 1], cha[:, t, :], ALU.mult, ALU.add)
            finish(0, zfa[:], 0, HALF, True)
            pb = held("pbb", [P, TILES, HALF], F32, 1)
        else:
            pb = new("pbb", [P, TILES, HALF], F32)
        for a, b in [(256, 384), (384, 512)]:
            for t in range(TILES):
                fetch(pb[:, t, a - HALF : b - HALF], t, l_n2, a, b)
        for h, (a, b) in enumerate([(256, 384), (384, 512)]):
            w = b - a
            js = slice(a - HALF, b - HALF)
            hj, lp, zf = [new("%sc%d" % (nm, h), [P, TILES, w], F32) for nm in ("hj", "lp", "zf")]
            nc.vector.tensor_tensor(hj[:], hi[:, :, js], pb[:, :, js], ALU.max)
            nc.vector.tensor_tensor(lp[:], lo[:, :, js], pb[:, :, js], ALU.min)
            nc.vector.scalar_tensor_tensor(zf[:], lp[:], -0.5, hj[:], ALU.mult, ALU.add)
            finish(h + 1, zf[:], a, b, False)

        out_rows = out.rearrange("(g t q) j -> t g q j", t=TILES, q=16)
        for t in range(TILES):
            leave(t, 384 if t < EARLY else HALF, S)
            for h, (c, d) in enumerate([(0, 256), (256, 384), (384, 512)] if t == TILES - 1 else [(0, 256), (256, 512)]):
                js = slice(c, d)
                ls = slice(c // 16, d // 16)
                prod = new("prod%d%d" % (t, h), [P, d - c], F32)
                far = new("far%d%d" % (t, h), [P, d - c], F32)
                res = new("res%d%d" % (t, h), [P, d - c], F32)
                if (t, h) in ():
                    near = new("near%d%d" % (t, h), [P, d - c], F32)
                    nc.scalar.activation(near[:], sg[t][:].indirect(l_n4[:, ls]), ACT.Copy)
                    nc.vector.tensor_tensor(prod[:], near[:], ah[t][:, js], ALU.mult)
                else:
                    nc.vector.tensor_tensor(prod[:], sg[t][:].indirect(l_n4[:, ls]), ah[t][:, js], ALU.mult)
                nc.scalar.activation(far[:], ah[t][:].indirect(l_n3[:, ls]), ACT.Copy)
                nc.vector.scalar_tensor_tensor(res[:], prod[:], -2.0, far[:], ALU.mult, ALU.add)
                nc.sync.dma_start(out_rows[t][:, :, js], res[:])
